import numpy as np, ml_dtypes
CORES = [113,118,241,246]
N = 4
BF = ml_dtypes.bfloat16
def gentries(a):
    return np.ascontiguousarray(a.reshape(8, 16, -1).transpose(0, 2, 1)).reshape(8, -1)
def gtable(e):
    e = np.asarray(e); return np.ascontiguousarray(e.reshape(8, -1, 16).transpose(0, 2, 1)).reshape(128, -1).astype(np.int32)
P, S, C, R = 1792, 48, 128, 4
def members(v):
    return np.stack([gentries(u) for u in v]).reshape(N, 8, R, N, C)
def pack(x, w, a, b):
    return {"fld": x.reshape(N, 128, P).astype(np.float32).astype(BF), "law": w.reshape(N, 128, S * S).astype(np.float32).astype(BF),
            "la": np.stack([gtable(u.reshape(8, -1)) for u in a]), "lb": np.stack([gtable(u.reshape(8, -1)) for u in b])}
def cut(p):
    return p[..., :N * C].reshape(N, 8, R, N, C), p[..., N * C:2 * N * C].reshape(N, 8, R, N, C)
def raw(rng):
    x = rng.integers(-128, 129, (N, 8, 16, P)); x[:, :, 0] = rng.integers(0, S, (N, 8, P))
    w = rng.integers(-16, 17, (N, 8, 16, S * S)); w[:, :, :2] = rng.integers(0, S, (N, 8, 2, S * S))
    a, b = cut(rng.permuted(np.tile(np.arange(P), (N, 8, R, 1)), axis=-1))
    return x, w, a, b
def setup_inputs(rng):
    return pack(*raw(rng))
def setup_inputs_swap(rng):
    x, w, a, b = raw(rng); a2, b2 = a.copy(), b.copy()
    for t in range(R):
        a2[:, :, t], b2[:, :, t] = (a[:, :, 0], b[:, :, 0]) if t % 2 == 0 else (b[:, :, 0], a[:, :, 0])
    return pack(x, w, a2, b2)
def setup_inputs_ends(rng):
    x, w, a, b = raw(rng); x[:, :, 0] = (S - 1) * rng.integers(0, 2, (N, 8, P)); w[:, :, :2] = (S - 1) * rng.integers(0, 2, (N, 8, 2, S * S))
    x[:, :, 1:] = 256 * rng.integers(0, 2, (N, 8, 15, P)) - 128; w[:, :, 2:] = 32 * rng.integers(0, 2, (N, 8, 14, S * S)) - 16
    w[:, :, 2::2] = 32 * rng.integers(0, 2, (N, 8, 7, 1)) - 16
    p = np.concatenate([np.arange(N * C), np.arange(P)[::-1][:N * C]])
    a, b = cut(np.tile(p, (N, 8, R, 1))); return pack(x, w, a, b)
def setup_inputs_one(rng):
    x, w, a, b = raw(rng); x[:, :, 0] = rng.integers(0, S, (N, 8, 1)); return pack(x, w, a, b)
def setup_inputs_spread(rng):
    x, w, a, b = raw(rng)
    x[:, :, 0] = np.floor(S * rng.random((N, 8, P)) ** 3); w[:, :, :2] = np.floor(S * rng.random((N, 8, 2, S * S)) ** 3)
    x[:, :, 1:] = np.floor(np.exp2(7 * rng.random((N, 8, 15, P)))) * rng.choice(np.array([-1, 0, 1]), (N, 8, 15, P))
    w[:, :, 2:] = np.floor(np.exp2(4 * rng.random((N, 8, 14, S * S)))) * rng.choice(np.array([-1, 0, 0, 1]), (N, 8, 14, S * S))
    a, b = cut(np.argsort(rng.random((N, 8, R, P)) + 2 * rng.random((N, 8, 1, P)), axis=-1)); return pack(x, w, a, b)
def check_inputs(d):
    bad = []; x = np.asarray(d["fld"]).astype(np.float32).reshape(N, 8, 16, P); w = np.asarray(d["law"]).astype(np.float32).reshape(N, 8, 16, S * S)
    if not ((x == np.floor(x)).all() and (x[:, :, 0] >= 0).all() and (x[:, :, 0] < S).all() and (np.abs(x[:, :, 1:]) <= 128).all()): bad.append("fields")
    if not ((w == np.floor(w)).all() and (w[:, :, :2] >= 0).all() and (w[:, :, :2] < S).all() and (np.abs(w[:, :, 2:]) <= 16).all()): bad.append("law")
    e = np.sort(np.concatenate([members(d["la"]).reshape(N, 8, R, N * C), members(d["lb"]).reshape(N, 8, R, N * C)], -1), -1)
    if not ((e >= 0).all() and (e < P).all()): bad.append("range")
    if not (e[..., 1:] > e[..., :-1]).all(): bad.append("disjoint")
    return bad
def reference(fld, law, la, lb):
    x = fld.astype(np.float32).astype(np.int64).reshape(N, 8, 16, P); w = law.astype(np.float32).astype(np.int64).reshape(N, 8, 16, S * S)
    a, b = members(la), members(lb)
    for t in range(R):
        for r in range(N):
            for q in range(N):
                for g in range(8):
                    u, v = x[r, g], x[q, g]; i, j = a[r, g, t, q], b[q, g, t, r]
                    col = w[r, g][:, u[0, i] * S + v[0, j]]
                    u[0, i] = col[0]; v[0, j] = col[1]
                    u[2:, i] += col[2:]; v[2:, j] -= col[2:]
    return {"y": x.reshape(N, 128, P).astype(np.float32)}

@@ -1,0 +1,373 @@
+from concourse.bass import DstId, RemoteDMATransfer
+from concourse.mybir import AluOpType as Op, ActivationFunctionType as Act
+
+P, LW, E, H = 1792, 2304, 1024, 512
+FULL = True
+PIECES = {"r": (0, 512), "m1": (512, 1536), "m2": (1536, LW)}
+OUT = [640, 1152]
+SCRATCH = {
+    "LI": ("sbuf", [128, 256], "int32"), "LU": ("sbuf", [128, 256], "uint16"),
+    "NI": ("sbuf", [128, 144], "float32"), "PI": ("sbuf", [128, 8], "int32"), "COL": ("sbuf", [128, 32], "float32"),
+    "HK": ("sbuf", [128, 48], "bfloat16"), "WK": ("sbuf", [128, 432], "float32"),
+    "ZS": ("sbuf", [128, 144], "bfloat16"), "ZP": ("sbuf", [128, 144], "bfloat16"),
+    "MM": ("sbuf", [128, 128], "bfloat16"), "MF": ("sbuf", [128, 128], "bfloat16"), "MS": ("sbuf", [128, 128], "bfloat16"),
+    "PT": ("sbuf", [128, P], "bfloat16"), "SRC": ("sbuf", [128, E], "bfloat16"),
+    "TB": ("sbuf", [128, 2 * LW], "bfloat16"), "LA": ("sbuf", [128, 4 * LW], "bfloat16"),
+    "TD": ("dram", [4, 128, 144], "bfloat16"),
+    "SP": ("sbuf", [128, P + 4 * E], "bfloat16"), "AB": ("sbuf", [128, P + 4 * E], "bfloat16"),
+    "GS": ("sbuf", [128, E], "bfloat16"), "GP": ("sbuf", [128, E], "bfloat16"), "PRE": ("sbuf", [128, E], "bfloat16"),
+    "MSG": ("sbuf", [128, 256], "float32"), "RCV": ("sbuf", [128, 256], "float32"), "OWN": ("sbuf", [128, 128], "float32"),
+    "IXF": ("sbuf", [128, 256], "float32"), "IX": ("sbuf", [128, 256], "uint16"), "PTR": ("sbuf", [128, 368], "uint16"),
+    "RC": ("sbuf", [128, 4 * H], "bfloat16"), "YO": ("sbuf", [128, P], "float32"),
+    "QS": ("psum", [128, 512], "float32"), "QP": ("psum", [128, 512], "float32"), "QF": ("psum", [128, 512], "float32"),
+    "QG": ("psum", [128, 512], "float32"), "QH": ("psum", [128, 512], "float32"),
+    "QI": ("psum", [128, 512], "float32"), "QJ": ("psum", [128, 512], "float32"),
+}
+SEMAPHORES = (["qv", "qa", "qt", "qg", "sent", "tab", "laws"] + ["m%d" % t for t in range(4)] + ["c%d" % t for t in range(4)]
+              + ["h" + k for k in PIECES] + ["d%d" % k for k in range(24)])
+
+
+def engine_sets(src, dsts, topo):
+    here = topo.cores_of(src)
+    out, used = {}, []
+    for group in ([d for d in dsts if d not in here], [d for d in dsts if d in here]):
+        for k, d in enumerate(group):
+            free = [e for e in topo.engines(src, d) if e not in used]
+            n = 1
+            while 2 * n * len(group) <= len(free):
+                n *= 2
+            out[d] = free[k * n:(k + 1) * n]
+        used = used + sum([out[d] for d in group], [])
+    return out
+
+
+def law_route(src, cores, topo):
+    near = [c for c in cores if c != src and c in topo.cores_of(src)]
+    far = [c for c in cores if c not in topo.cores_of(src)]
+    relay = [c for c in topo.cores_of(far[0]) if c not in cores and topo.die(c) == topo.die(src)][0]
+    return near, relay, far
+
+
+def fused(g, T, topo, core, sets, sem, src, dst):
+    tr = []
+    for d in sets:
+        rid, pid = topo.addr(d, core)
+        tr.append(RemoteDMATransfer(dst_ids=[DstId(rid=rid, pnc=pid)], dma_engine_mask=sum(1 << e for e in sets[d]),
+                                    remote_sem=T.sem[sem(d)], src=src(d), dst=dst))
+    g.remote_dma_fused(tr, local_sem=T.sem.sent)
+    return sum(len(s) for s in sets.values())
+
+
+def rank_program(g, core, T, topo):
+    me = T.rank_of(core)
+    cores = list(T.cores)
+    routes = [law_route(c, cores, topo) for c in cores]
+    if me is None:
+        total = 0
+        for x in range(4):
+            near, relay, far = routes[x]
+            if FULL and relay == core:
+                for k, (a, b) in PIECES.items():
+                    g.wait_ge(T.sem["h" + k], len(engine_sets(cores[x], near + [relay], topo)[core]))
+                    part = T.LA[:, LW * x + a:LW * x + b]
+                    total += fused(g, T, topo, core, engine_sets(core, far, topo), lambda d: "laws", lambda d: part, part)
+        if total:
+            g.wait_ge(T.sem.sent, total)
+        return
+    peers = [x for x in range(4) if x != me]
+    sets = engine_sets(core, [cores[x] for x in peers], topo)
+    arrive = sum(len(engine_sets(cores[x], [c for c in cores if c != cores[x]], topo)[core]) for x in peers)
+    Q = {"v": g.vector, "a": g.scalar, "t": g.tensor, "g": g, "s": g.sync}
+    count, waited, writes, reads, banks, ndma = {}, {}, [], [], [], [0]
+
+    def v(name, a, b, step=1):
+        return (T[name][:, a:b] if step == 1 else T[name][:, a:b:step], (name, a, b, step))
+
+    def reg(name, a, b):
+        return (name, a, b, 1)
+
+    def hit(r, s):
+        if r[0] != s[0] or (r[3] == s[3] > 1 and (r[1] - s[1]) % r[3]):
+            return False
+        return r[0][0] == "Q" or (r[1] < s[2] and s[1] < r[2])
+
+    def wait(q, tok):
+        if waited.get((q, tok[0]), 0) < tok[1]:
+            waited[(q, tok[0])] = tok[1]
+            Q[q].wait_ge(T.sem[tok[0]], tok[1])
+
+    def before(q, rd, wr):
+        need = {}
+        for earlier, mine in ((writes, rd + wr), (reads, wr), ([b for b in banks if b[1][0] != "q" + q], rd)):
+            for r, tok in earlier:
+                if any(hit(r, s) for s in mine):
+                    need[tok[0]] = max(need.get(tok[0], 0), tok[1])
+        for s in sorted(need):
+            wait(q, (s, need[s]))
+
+    def note(tok, rd, wr):
+        writes.extend((r, tok) for r in wr)
+        reads.extend((r, tok) for r in rd)
+        banks.extend((r, tok) for r in rd if r[0][0] == "Q")
+
+    def done(q, ins, rd, wr):
+        count["q" + q] = count.get("q" + q, 0) + 1
+        ins.then_inc(T.sem["q" + q], 1)
+        note(("q" + q, count["q" + q]), rd, wr)
+
+    def regs(*xs):
+        return [r for x in xs if isinstance(x, tuple) for r in x[1:]]
+
+    def ap(x):
+        return x[0] if isinstance(x, tuple) else x
+
+    def ind(win, off):
+        return (win[0].indirect(off[0]), win[1], off[1])
+
+    def ts(out, in0, s1, s2, op0, op1=None):
+        before("v", regs(in0, s1, s2), regs(out))
+        args = (ap(out), ap(in0), ap(s1), ap(s2), op0) + (() if op1 is None else (op1,))
+        done("v", g.vector.tensor_scalar(*args), regs(in0, s1, s2), regs(out))
+
+    def tt(out, a, b, op):
+        before("v", regs(a, b), regs(out))
+        done("v", g.vector.tensor_tensor(ap(out), ap(a), ap(b), op), regs(a, b), regs(out))
+
+    def cp(q, out, in_, scale=None, bias=None, func=Act.Identity):
+        if q == "v" and scale is not None:
+            return ts(out, in_, scale, None, Op.mult)
+        if q == "v" and bias is not None:
+            return ts(out, in_, bias, None, Op.add)
+        rd = regs(in_, scale, bias)
+        before(q, rd, regs(out))
+        if q == "v":
+            ins = g.vector.tensor_copy(ap(out), ap(in_))
+        else:
+            ins = g.scalar.activation(ap(out), ap(in_), func, 0.0 if bias is None else ap(bias),
+                                      1.0 if scale is None else ap(scale))
+        done(q, ins, rd, regs(out))
+
+    def scatter(win, off, in_):
+        before("v", regs(off, in_), regs(win))
+        done("v", g.vector.tensor_copy(win[0].indirect(off[0]), in_[0]), regs(off, in_), regs(win))
+
+    def mm(items, first=True, last=True):
+        if first:
+            before("t", [], regs(items[0][0]))
+        for k, (out, lhs, rhs) in enumerate(items):
+            before("t", regs(lhs, rhs), [])
+            ins = g.tensor.matmul(out[0], lhs[0], rhs[0], first and k == 0, last and k == len(items) - 1)
+        done("t", ins, regs(*[x for p in items for x in p[1:]]), [reg(items[0][0][1][0], 0, 512)])
+
+    def to_list(out, z, name, a, b):
+        mm([(out, v(z, 15 - i, 143 - i), v(name, a + i, b, 16)) for i in range(16)])
+
+    def dma(q, out, in_, rd, wr, ordered=True):
+        if ordered:
+            before(q, rd, wr)
+        s = "d%d" % ndma[0]
+        ndma[0] += 1
+        Q[q].dma_start(out, in_).then_inc(T.sem[s], 16)
+        count[s] = 16
+        note((s, 16), rd, wr)
+
+    def piece(key):
+        if FULL and key in PIECES:
+            near, relay, far = routes[me]
+            part = v("LA", LW * me + PIECES[key][0], LW * me + PIECES[key][1])
+            before("g", regs(part), [])
+            count["sent"] += fused(g, T, topo, core, engine_sets(core, near + [relay], topo),
+                                   lambda d: "h" + key if d == relay else "laws", lambda d: part[0], part[0])
+
+    def send(sem, src, dst, rd, landing):
+        before("g", rd, [])
+        count["sent"] = count.get("sent", 0) + fused(g, T, topo, core, sets, lambda d: sem, lambda d: src(cores.index(d)), dst)
+        count[sem] = arrive
+        note((sem, arrive), [], landing)
+        piece(sem)
+
+    def iota(out, pattern, base, mult):
+        before("g", [], regs(out))
+        done("g", g.iota(out[0], pattern, base, mult, allow_small_or_imprecise_dtypes=True), [], regs(out))
+
+    col = lambda k: v("COL", k, k + 1)
+    hk = lambda k: v("HK", k, k + 1)
+    raw = lambda t, h: v("LU", 128 * h + 32 * t, 128 * h + 32 * t + 32)
+    ptr = lambda t, h: raw(0, h) if t == 0 else v("PTR", 64 * t + 32 * h, 64 * t + 32 * h + 32)
+    src = lambda t, h: v("SRC", H * h, H * h + H) if t == 0 else v("TB", E * (t - 1) + H * h, E * (t - 1) + H * h + H)
+    at = lambda t: P + E * t
+    law = v("LA", LW * me, LW * me + LW)
+    LAST = (("QF", "MF", "v", 0), ("QG", "MS", "a", H), ("QI", "MF", "v", 256), ("QJ", "MS", "a", H + 256))
+    EQ, PM, NP, NC, W01, WP, NE0, NE1, NT, WS = 0, 4, 8, 12, 13, 14, 15, 16, 17, 18
+
+    dma("s", T.LI[:, 0:128], T.la[:], [], [reg("LI", 0, 128)])
+    dma("a", T.TD[me], T.law[1::16, :], [], [reg("TD", me, me + 1)])
+    dma("a", T.LI[:, 128:256], T.lb[:], [], [reg("LI", 128, 256)])
+    done("v", g.vector.memset(T.SP[:, 0:P], 0.0), [], [reg("SP", 0, P)])
+    done("g", g.iota(T.PI[:, 0:1], [[0, 1]], 0, 1), [], [reg("PI", 0, 1)])
+    iota(v("NI", 0, 144), [[1, 144]], 0, 0)
+    iota(v("COL", NP, NP + 2), [[-15, 2]], 0, -1)
+    iota(v("TB", 3 * E, 3 * E + H), [[0, H]], 0, 0)
+    dma("s", T.SP[0::16, 0:P], T.fld[0::16, :], [], [reg("SP", 0, P)])
+    dma("s", law[0], T.law[:], [], regs(law))
+    send("tab", lambda x: T.TD[me], T.TD[me], [reg("TD", me, me + 1)], [reg("TD", x, x + 1) for x in peers])
+    iota(v("TB", 3 * E + H, 2 * LW), [[0, E]], 0, 0)
+    ts(v("PI", 4, 5), v("PI", 0, 1), 15, None, Op.bitwise_and)
+    cp("v", col(PM), v("PI", 4, 5))
+    ts(v("COL", 0, 4), v("NI", 0, 4), col(PM), None, Op.is_equal)
+    cp("a", v("HK", 0, 48), v("NI", 0, 48), scale=col(EQ + 3))
+    cp("v", v("PT", 0, 128), v("NI", 0, 128), scale=col(EQ + 2))
+    cp("a", col(NC), col(PM), bias=col(NP + 1))
+    cp("a", col(W01), col(EQ), bias=col(EQ + 1))
+    cp("a", v("WK", 0, 144), v("NI", 0, 144), bias=col(NC), func=Act.Abs)
+    cp("a", v("ZS", 0, 144), v("WK", 0, 144), scale=-1.0, bias=col(W01), func=Act.Relu)
+    for k in (1, 2, 4):
+        cp("v", v("PT", 128 * k, 256 * k), v("PT", 0, 128 * k), bias=hk(k))
+    cp("a", v("PT", E, P), v("PT", 0, P - E), bias=hk(8))
+    cp("v", v("SRC", 0, E), v("PT", 0, E), bias=hk(at(0) // 128))
+    cp("v", v("LU", 0, 128), v("LI", 0, 128))
+    cp("v", v("LU", 128, 256), v("LI", 128, 256))
+
+    def gather2(name, win, lists):
+        for h, q in enumerate("va"):
+            cp(q, v(name, H * h, H * h + H), ind(win, lists(h)))
+
+    def message(t):
+        b = 64 * t
+        cp("a", v("MSG", b, b + 64, 2), v("QS", 32, 64))
+        cp("a", v("MSG", b + 1, b + 64, 2), v("QS", 0, 32), scale=48.0, bias=float(LW * (me if FULL and t == 3 else me % 2)))
+        send("m%d" % t, lambda x: T.MSG[:, b + 16 * x:b + 16 * x + 16], T.RCV[:, b + 16 * me:b + 16 * me + 16],
+             [reg("MSG", b, b + 64)], [reg("RCV", b + 16 * x, b + 16 * x + 16) for x in peers])
+        cp("a", v("RCV", b + 16 * me, b + 16 * me + 16), v("MSG", b + 16 * me, b + 16 * me + 16))
+        cp("a", v("OWN", 32 * t, 32 * t + 32), v("QS", 0, 32), scale=48.0)
+
+    def state(q, t, h):
+        cp(q, v("PRE", H * h, H * h + H), ind(v("AB", 0, at(t)), ptr(t, h)))
+
+    def kept(h, bank):
+        return (v(bank, 0, H), v("MM", 0, 128), v("PRE", H * h, H * h + H))
+
+    def lookup(t):
+        b, c = 64 * t, at(t)
+        tt(v("IXF", b, b + 32), v("OWN", 32 * t, 32 * t + 32), v("RCV", b, b + 64, 2), Op.add)
+        if t < 3 or FULL:
+            tt(v("IXF", b + 32, b + 64), v("RCV", b + 1, b + 64, 2), v("MSG", b, b + 64, 2), Op.add)
+            cp("v", v("IX", b, b + 64), v("IXF", b, b + 64))
+        else:
+            cp("v", v("IX", b, b + 32), v("IXF", b, b + 32))
+        if t < 3:
+            cp("v", v("SP", c, c + H), ind(law, v("IX", b, b + 32)), scale=col(NE1))
+            for k in range(2):
+                cp("a", v("SP", c + H + 256 * k, c + H + 256 * k + 256),
+                   ind(v("TB", 0, 2 * LW), v("IX", b + 32 + 16 * k, b + 48 + 16 * k)), scale=col(EQ + k))
+        elif FULL:
+            for k in range(2):
+                cp("v", v("SP", c + 256 * k, c + 256 * k + 256), ind(law, v("IX", b + 16 * k, b + 16 * k + 16)))
+                cp("a", v("SP", c + H + 256 * k, c + H + 256 * k + 256),
+                   ind(v("LA", 0, 4 * LW), v("IX", b + 32 + 16 * k, b + 48 + 16 * k)))
+            return
+        else:
+            cp("v", v("SP", c, c + 256), ind(law, v("IX", b, b + 16)))
+            cp("a", v("SP", c + 256, c + H), ind(law, v("IX", b + 16, b + 32)))
+        send("c%d" % t, lambda x: T.SP[:, c + 128 * x:c + 128 * x + 128], T.RC[:, H * t + 128 * me:H * t + 128 * me + 128],
+             [reg("SP", c, c + H)], [reg("RC", H * t + 128 * x, H * t + 128 * x + 128) for x in peers])
+
+    def own_columns(q, t):
+        cp(q, v("RC", H * t + 128 * me, H * t + 128 * me + 128), v("SP", at(t) + 128 * me, at(t) + 128 * me + 128))
+
+    if FULL:
+        n = 0
+        for x in peers:
+            near, relay, far = routes[x]
+            n += len(engine_sets(cores[x], near + [relay], topo)[core] if core in near else engine_sets(relay, far, topo)[core])
+        count["laws"] = n * len(PIECES)
+        note(("laws", count["laws"]), [], [reg("LA", LW * x, LW * x + LW) for x in peers])
+
+    for t in range(4):
+        gather2("GS", v("SP", 0, at(t)), lambda h: ptr(t, h))
+        to_list(v("QS", 0, 64), "ZS", "GS", 0, E)
+        if t == 0:
+            cp("v", v("TB", 0, E), v("SRC", 0, E), bias=hk(8))
+            cp("a", v("TB", E, 2 * E), v("SRC", 0, E), bias=hk(16))
+        else:
+            state("a", t - 1, 0)
+        message(t)
+        if t > 0:
+            own_columns("a", t - 1)
+        scatter(v("PT", 0, P), raw(t, 0), src(t, 0))
+        scatter(v("PT", 0, P), raw(t, 1), src(t, 1))
+        if t == 0:
+            cp("a", v("TB", 2 * E, 3 * E), v("SRC", 0, E), bias=hk(24))
+            before("s", [], [reg("TB", 0, 2 * LW)])
+            slot = lambda x: T.TB[x // 2::16, LW * (x % 2):LW * (x % 2) + LW]
+            rs = lambda x: [reg("TB", LW * (x % 2), LW * (x % 2) + LW)]
+            dma("s", slot(me), T.law[1::16, :], [], rs(me), ordered=False)
+            before("s", [reg("TD", 0, 4)], [])
+            for x in peers:
+                dma("s", slot(x), T.TD[x], [reg("TD", x, x + 1)], rs(x), ordered=False)
+            before("g", [reg("TB", 0, 2 * LW)], [])
+            piece("r")
+            dma("s", T.AB[:, 0:P], T.fld[:], [], [reg("AB", 0, P)])
+            cp("a", col(WP), col(EQ + 3), scale=128.0, bias=col(EQ + 2))
+            cp("a", col(NE1), col(EQ + 1), scale=-1.0, bias=1.0)
+            cp("a", v("ZP", 0, 144), v("WK", 0, 144), scale=-128.0, bias=col(WP), func=Act.Relu)
+            cp("a", col(NE0), col(EQ), scale=-1.0, bias=1.0)
+            cp("a", col(NT), col(EQ + 1), bias=col(NP))
+            cp("a", v("WK", 144, 272), v("NI", 0, 128), bias=col(NP), func=Act.Abs)
+            cp("a", col(WS), col(EQ + 1), scale=2.0, bias=col(EQ))
+            cp("a", v("WK", 272, 400), v("NI", 0, 128), bias=col(NT), func=Act.Abs)
+            cp("a", col(WS + 1), col(WS), bias=-1.0)
+            cp("a", v("MM", 0, 128), v("WK", 144, 272), scale=-1.0, bias=col(NE0), func=Act.Relu)
+        else:
+            c = at(t - 1)
+            mm([kept(0, "QF"), (v("QF", 0, H), v("MF", 0, 128), v("SP", c, c + H))])
+            state("a", t - 1, 1)
+            mm([(v("QG", 0, H), v("ZS", 15, 143), v("SP", c + H, c + E)), kept(1, "QG"),
+                (v("QG", 0, H), v("MS", 0, 128), v("RC", H * (t - 1), H * t))])
+            cp("a", v("AB", c, c + H), v("QF", 0, H))
+        if t < 3:
+            gather2("GP", v("PT", 0, P), lambda h: raw(t + 1, h))
+            to_list(v("QP", 0, 64), "ZP", "GP", 0, E)
+        if t == 0:
+            cp("a", v("MF", 0, 128), v("WK", 144, 272), scale=-1.0, bias=col(NE1), func=Act.Relu)
+            cp("a", v("WK", 272, 400), v("WK", 272, 400), scale=-1.0, bias=1.0, func=Act.Relu)
+            cp("a", v("MS", 0, 128), v("WK", 272, 400), scale=col(WS + 1))
+        else:
+            cp("a", v("AB", c + H, c + E), v("QG", 0, H))
+        if t == 3:
+            to_list(v("QP", 0, 56), "ZP", "PT", 0, P // 2)
+            if FULL:
+                gather2("PRE", v("AB", 0, at(3)), lambda h: ptr(3, h))
+                for bank, m, q, o in LAST:
+                    mm([(v(bank, 0, 256), v("MM", 0, 128), v("PRE", o, o + 256))], last=False)
+            else:
+                to_list(v("QH", 0, 56), "ZP", "PT", P // 2, P)
+        lookup(t)
+        if t < 3:
+            cp("v", v("PTR", 64 * t + 64, 64 * t + 128), v("QP", 0, 64))
+
+    c = at(3)
+    cp("v", v("PTR", 256, 312), v("QP", 0, 56))
+    if FULL:
+        for bank, m, q, o in LAST:
+            mm([(v(bank, 0, 256), v(m, 0, 128), v("SP", c + o, c + o + 256))], first=False)
+            cp(q, v("AB", c + o, c + o + 256), v(bank, 0, 256))
+        to_list(v("QH", 0, 56), "ZP", "PT", P // 2, P)
+    else:
+        own_columns("v", 3)
+        gather2("PRE", v("AB", 0, at(3)), lambda h: ptr(3, h))
+        mm([kept(0, "QF"), (v("QF", 0, H), v("MF", 0, 128), v("SP", c, c + H))])
+        mm([kept(1, "QG")], last=False)
+        cp("a", v("AB", c, c + H), v("QF", 0, H))
+        mm([(v("QG", 0, H), v("MS", 0, 128), v("RC", 3 * H, 4 * H))], first=False)
+        cp("a", v("AB", c + H, c + E), v("QG", 0, H))
+    o = 0
+    for w in OUT:
+        if o <= P // 2 < o + w:
+            cp("v", v("PTR", 312, 368), v("QH", 0, 56))
+        for q, a in (("v", o), ("a", o + w // 2)):
+            cp(q, v("YO", a, a + w // 2), ind(v("AB", 0, at(4)), v("PTR", 256 + a // 16, 256 + (a + w // 2) // 16)))
+        dma("s", T.y[:, o:o + w], T.YO[:, o:o + w], [reg("YO", o, o + w)], [])
+        o += w
+    for s in sorted(count):
+        wait("g", (s, count[s]))

@@ -2,29 +2,24 @@ from concourse.bass import DstId, RemoteDMATransfer
 from concourse.mybir import AluOpType as Op, ActivationFunctionType as Act
 
 P, LW, E, H = 1792, 2304, 1024, 512
-FULL = True
 PIECES = {"r": (0, 512), "m1": (512, 1536), "m2": (1536, LW)}
-OUT = [640, 1152]
+OUT = [384, 512, 896]
+S, B, F = "sbuf", "bfloat16", "float32"
 SCRATCH = {
-    "LI": ("sbuf", [128, 256], "int32"), "LU": ("sbuf", [128, 256], "uint16"),
-    "NI": ("sbuf", [128, 144], "float32"), "PI": ("sbuf", [128, 8], "int32"), "COL": ("sbuf", [128, 32], "float32"),
-    "HK": ("sbuf", [128, 48], "bfloat16"), "WK": ("sbuf", [128, 432], "float32"),
-    "ZS": ("sbuf", [128, 144], "bfloat16"), "ZP": ("sbuf", [128, 144], "bfloat16"),
-    "MM": ("sbuf", [128, 128], "bfloat16"), "MF": ("sbuf", [128, 128], "bfloat16"), "MS": ("sbuf", [128, 128], "bfloat16"),
-    "PT": ("sbuf", [128, P], "bfloat16"), "SRC": ("sbuf", [128, E], "bfloat16"),
-    "TB": ("sbuf", [128, 2 * LW], "bfloat16"), "LA": ("sbuf", [128, 4 * LW], "bfloat16"),
-    "TD": ("dram", [4, 128, 144], "bfloat16"),
-    "SP": ("sbuf", [128, P + 4 * E], "bfloat16"), "AB": ("sbuf", [128, P + 4 * E], "bfloat16"),
-    "GS": ("sbuf", [128, E], "bfloat16"), "GP": ("sbuf", [128, E], "bfloat16"), "PRE": ("sbuf", [128, E], "bfloat16"),
-    "MSG": ("sbuf", [128, 256], "float32"), "RCV": ("sbuf", [128, 256], "float32"), "OWN": ("sbuf", [128, 128], "float32"),
-    "IXF": ("sbuf", [128, 256], "float32"), "IX": ("sbuf", [128, 256], "uint16"), "PTR": ("sbuf", [128, 368], "uint16"),
-    "RC": ("sbuf", [128, 4 * H], "bfloat16"), "YO": ("sbuf", [128, P], "float32"),
-    "QS": ("psum", [128, 512], "float32"), "QP": ("psum", [128, 512], "float32"), "QF": ("psum", [128, 512], "float32"),
-    "QG": ("psum", [128, 512], "float32"), "QH": ("psum", [128, 512], "float32"),
-    "QI": ("psum", [128, 512], "float32"), "QJ": ("psum", [128, 512], "float32"),
+    "LI": (S, [128, 4, 32], "int32"), "LJ": (S, [128, 4, 32], "int32"), "LU": (S, [128, 4, 64], "uint16"),
+    "NI": (S, [128, 144], F), "PI": (S, [128, 8], "int32"),
+    "COL": (S, [128, 32], F), "HK": (S, [128, 48], B), "WK": (S, [128, 144], F), "ZS": (S, [128, 144], B),
+    "ZP": (S, [128, 144], B), "MM": (S, [128, 128], B), "MF": (S, [128, 128], B), "MS": (S, [128, 128], B),
+    "MI": (S, [128, 128], B), "PT": (S, [128, P], B), "SRC": (S, [128, E], B), "HI": (S, [128, E], B),
+    "TB": (S, [128, 2 * LW], B), "LA": (S, [128, 4 * LW], B), "TD": ("dram", [4, 128, 144], B),
+    "SP": (S, [128, P + 4 * E], B), "AB": (S, [128, P + 4 * E], B),
+    "GS": (S, [128, E], B), "GP": (S, [128, E], B), "PRE": (S, [128, E], B),
+    "MSG": (S, [128, 256], F), "RCV": (S, [128, 256], F), "OWN": (S, [128, 128], F), "IXF": (S, [128, 256], F),
+    "IX": (S, [128, 256], "uint16"), "PTR": (S, [128, 368], "uint16"), "RC": (S, [128, 3 * H], B), "YO": (S, [128, P], F),
 }
-SEMAPHORES = (["qv", "qa", "qt", "qg", "sent", "tab", "laws"] + ["m%d" % t for t in range(4)] + ["c%d" % t for t in range(4)]
-              + ["h" + k for k in PIECES] + ["d%d" % k for k in range(24)])
+SCRATCH.update({"Q" + k: ("psum", [128, 512], F) for k in "SPFGHIJ"})
+SEMAPHORES = (["qv", "qa", "qt", "qg", "sent", "tab", "laws"] + ["m%d" % t for t in range(4)] + ["c%d" % t for t in range(3)]
+              + ["h" + k for k in PIECES] + ["d%d" % k for k in range(20)])
 
 
 def engine_sets(src, dsts, topo):
@@ -66,7 +61,7 @@ def rank_program(g, core, T, topo):
         total = 0
         for x in range(4):
             near, relay, far = routes[x]
-            if FULL and relay == core:
+            if relay == core:
                 for k, (a, b) in PIECES.items():
                     g.wait_ge(T.sem["h" + k], len(engine_sets(cores[x], near + [relay], topo)[core]))
                     part = T.LA[:, LW * x + a:LW * x + b]
@@ -124,10 +119,9 @@ def rank_program(g, core, T, topo):
     def ind(win, off):
         return (win[0].indirect(off[0]), win[1], off[1])
 
-    def ts(out, in0, s1, s2, op0, op1=None):
+    def ts(out, in0, s1, s2, op0):
         before("v", regs(in0, s1, s2), regs(out))
-        args = (ap(out), ap(in0), ap(s1), ap(s2), op0) + (() if op1 is None else (op1,))
-        done("v", g.vector.tensor_scalar(*args), regs(in0, s1, s2), regs(out))
+        done("v", g.vector.tensor_scalar(ap(out), ap(in0), ap(s1), ap(s2), op0), regs(in0, s1, s2), regs(out))
 
     def tt(out, a, b, op):
         before("v", regs(a, b), regs(out))
@@ -172,7 +166,7 @@ def rank_program(g, core, T, topo):
         note((s, 16), rd, wr)
 
     def piece(key):
-        if FULL and key in PIECES:
+        if key in PIECES:
             near, relay, far = routes[me]
             part = v("LA", LW * me + PIECES[key][0], LW * me + PIECES[key][1])
             before("g", regs(part), [])
@@ -190,25 +184,31 @@ def rank_program(g, core, T, topo):
         before("g", [], regs(out))
         done("g", g.iota(out[0], pattern, base, mult, allow_small_or_imprecise_dtypes=True), [], regs(out))
 
+    def mark(out, in_, pattern, base, fill):
+        out, in_ = v(out, 0, 128), v(in_, 0, 128)
+        before("g", regs(in_), regs(out))
+        done("g", g.affine_select(out[0], in_[0], pattern, Op.not_equal, fill, base, 1), regs(in_), regs(out))
+
     col = lambda k: v("COL", k, k + 1)
     hk = lambda k: v("HK", k, k + 1)
-    raw = lambda t, h: v("LU", 128 * h + 32 * t, 128 * h + 32 * t + 32)
+    raw = lambda t, h, n=1: (T.LU[:, t, 32 * h:32 * (h + n)], reg("LU", h, h + n))
     ptr = lambda t, h: raw(0, h) if t == 0 else v("PTR", 64 * t + 32 * h, 64 * t + 32 * h + 32)
-    src = lambda t, h: v("SRC", H * h, H * h + H) if t == 0 else v("TB", E * (t - 1) + H * h, E * (t - 1) + H * h + H)
     at = lambda t: P + E * t
     law = v("LA", LW * me, LW * me + LW)
     LAST = (("QF", "MF", "v", 0), ("QG", "MS", "a", H), ("QI", "MF", "v", 256), ("QJ", "MS", "a", H + 256))
-    EQ, PM, NP, NC, W01, WP, NE0, NE1, NT, WS = 0, 4, 8, 12, 13, 14, 15, 16, 17, 18
+    EQ, PM, NP, NC, W01, WP, NE1, NE0 = 0, 4, 8, 12, 13, 14, 16, 17
+    diag, field = [[-1, 128]], [[-16, 8], [-200, 16]]
 
-    dma("s", T.LI[:, 0:128], T.la[:], [], [reg("LI", 0, 128)])
+    dma("s", T.LI[:], T.la[:], [], [reg("LI", 0, 1)])
     dma("a", T.TD[me], T.law[1::16, :], [], [reg("TD", me, me + 1)])
-    dma("a", T.LI[:, 128:256], T.lb[:], [], [reg("LI", 128, 256)])
+    dma("a", T.LJ[:], T.lb[:], [], [reg("LJ", 0, 1)])
     done("v", g.vector.memset(T.SP[:, 0:P], 0.0), [], [reg("SP", 0, P)])
     done("g", g.iota(T.PI[:, 0:1], [[0, 1]], 0, 1), [], [reg("PI", 0, 1)])
     iota(v("NI", 0, 144), [[1, 144]], 0, 0)
     iota(v("COL", NP, NP + 2), [[-15, 2]], 0, -1)
     iota(v("TB", 3 * E, 3 * E + H), [[0, H]], 0, 0)
     dma("s", T.SP[0::16, 0:P], T.fld[0::16, :], [], [reg("SP", 0, P)])
+    dma("s", T.TB[:, 2 * E:3 * E], T.law[:, 0:E], [], [reg("TB", 2 * E, 3 * E)])
     dma("s", law[0], T.law[:], [], regs(law))
     send("tab", lambda x: T.TD[me], T.TD[me], [reg("TD", me, me + 1)], [reg("TD", x, x + 1) for x in peers])
     iota(v("TB", 3 * E + H, 2 * LW), [[0, E]], 0, 0)
@@ -224,9 +224,8 @@ def rank_program(g, core, T, topo):
     for k in (1, 2, 4):
         cp("v", v("PT", 128 * k, 256 * k), v("PT", 0, 128 * k), bias=hk(k))
     cp("a", v("PT", E, P), v("PT", 0, P - E), bias=hk(8))
-    cp("v", v("SRC", 0, E), v("PT", 0, E), bias=hk(at(0) // 128))
-    cp("v", v("LU", 0, 128), v("LI", 0, 128))
-    cp("v", v("LU", 128, 256), v("LI", 128, 256))
+    cp("v", (T.LU[:, :, 0:32], reg("LU", 0, 1)), (T.LI[:], reg("LI", 0, 1)))
+    cp("v", (T.LU[:, :, 32:64], reg("LU", 1, 2)), (T.LJ[:], reg("LJ", 0, 1)))
 
     def gather2(name, win, lists):
         for h, q in enumerate("va"):
@@ -235,14 +234,17 @@ def rank_program(g, core, T, topo):
     def message(t):
         b = 64 * t
         cp("a", v("MSG", b, b + 64, 2), v("QS", 32, 64))
-        cp("a", v("MSG", b + 1, b + 64, 2), v("QS", 0, 32), scale=48.0, bias=float(LW * (me if FULL and t == 3 else me % 2)))
+        cp("a", v("MSG", b + 1, b + 64, 2), v("QS", 0, 32), scale=48.0, bias=float(LW * (me if t == 3 else me % 2)))
         send("m%d" % t, lambda x: T.MSG[:, b + 16 * x:b + 16 * x + 16], T.RCV[:, b + 16 * me:b + 16 * me + 16],
              [reg("MSG", b, b + 64)], [reg("RCV", b + 16 * x, b + 16 * x + 16) for x in peers])
-        cp("a", v("RCV", b + 16 * me, b + 16 * me + 16), v("MSG", b + 16 * me, b + 16 * me + 16))
+
+    def own_part(t):
+        b = 64 * t + 16 * me
+        cp("a", v("RCV", b, b + 16), v("MSG", b, b + 16))
         cp("a", v("OWN", 32 * t, 32 * t + 32), v("QS", 0, 32), scale=48.0)
 
-    def state(q, t, h):
-        cp(q, v("PRE", H * h, H * h + H), ind(v("AB", 0, at(t)), ptr(t, h)))
+    def state(q, t, h, scale=None):
+        cp(q, v("PRE", H * h, H * h + H), ind(v("AB", 0, at(t)), ptr(t, h)), scale=scale)
 
     def kept(h, bank):
         return (v(bank, 0, H), v("MM", 0, 128), v("PRE", H * h, H * h + H))
@@ -250,54 +252,53 @@ def rank_program(g, core, T, topo):
     def lookup(t):
         b, c = 64 * t, at(t)
         tt(v("IXF", b, b + 32), v("OWN", 32 * t, 32 * t + 32), v("RCV", b, b + 64, 2), Op.add)
-        if t < 3 or FULL:
-            tt(v("IXF", b + 32, b + 64), v("RCV", b + 1, b + 64, 2), v("MSG", b, b + 64, 2), Op.add)
-            cp("v", v("IX", b, b + 64), v("IXF", b, b + 64))
-        else:
-            cp("v", v("IX", b, b + 32), v("IXF", b, b + 32))
-        if t < 3:
-            cp("v", v("SP", c, c + H), ind(law, v("IX", b, b + 32)), scale=col(NE1))
-            for k in range(2):
-                cp("a", v("SP", c + H + 256 * k, c + H + 256 * k + 256),
-                   ind(v("TB", 0, 2 * LW), v("IX", b + 32 + 16 * k, b + 48 + 16 * k)), scale=col(EQ + k))
-        elif FULL:
+        tt(v("IXF", b + 32, b + 64), v("RCV", b + 1, b + 64, 2), v("MSG", b, b + 64, 2), Op.add)
+        cp("v", v("IX", b, b + 64), v("IXF", b, b + 64))
+        second = lambda k: (v("SP", c + H + 256 * k, c + H + 256 * k + 256), v("IX", b + 32 + 16 * k, b + 48 + 16 * k))
+        if t == 3:
             for k in range(2):
                 cp("v", v("SP", c + 256 * k, c + 256 * k + 256), ind(law, v("IX", b + 16 * k, b + 16 * k + 16)))
-                cp("a", v("SP", c + H + 256 * k, c + H + 256 * k + 256),
-                   ind(v("LA", 0, 4 * LW), v("IX", b + 32 + 16 * k, b + 48 + 16 * k)))
+                cp("a", second(k)[0], ind(v("LA", 0, 4 * LW), second(k)[1]))
             return
+        if t == 0:
+            for k, q in enumerate("va"):
+                cp(q, v("SP", c + 256 * k, c + 256 * k + 256), ind(law, v("IX", b + 16 * k, b + 16 * k + 16)), scale=col(NE1))
         else:
-            cp("v", v("SP", c, c + 256), ind(law, v("IX", b, b + 16)))
-            cp("a", v("SP", c + 256, c + H), ind(law, v("IX", b + 16, b + 32)))
+            cp("v", v("SP", c, c + H), ind(law, v("IX", b, b + 32)), scale=col(NE1))
+        for k, q in enumerate("va" if t == 0 else "aa"):
+            cp(q, second(k)[0], ind(v("TB", 0, 2 * LW), second(k)[1]), scale=col(EQ + k))
         send("c%d" % t, lambda x: T.SP[:, c + 128 * x:c + 128 * x + 128], T.RC[:, H * t + 128 * me:H * t + 128 * me + 128],
              [reg("SP", c, c + H)], [reg("RC", H * t + 128 * x, H * t + 128 * x + 128) for x in peers])
 
-    def own_columns(q, t):
-        cp(q, v("RC", H * t + 128 * me, H * t + 128 * me + 128), v("SP", at(t) + 128 * me, at(t) + 128 * me + 128))
-
-    if FULL:
-        n = 0
-        for x in peers:
-            near, relay, far = routes[x]
-            n += len(engine_sets(cores[x], near + [relay], topo)[core] if core in near else engine_sets(relay, far, topo)[core])
-        count["laws"] = n * len(PIECES)
-        note(("laws", count["laws"]), [], [reg("LA", LW * x, LW * x + LW) for x in peers])
+    n = 0
+    for x in peers:
+        near, relay, far = routes[x]
+        n += len(engine_sets(cores[x], near + [relay], topo)[core] if core in near else engine_sets(relay, far, topo)[core])
+    count["laws"] = n * len(PIECES)
+    note(("laws", count["laws"]), [], [reg("LA", LW * x, LW * x + LW) for x in peers])
 
     for t in range(4):
+        c = at(t - 1)
         gather2("GS", v("SP", 0, at(t)), lambda h: ptr(t, h))
+        if t > 0:
+            mm([(v("QF", 0, H), v("MF", 0, 128), v("SP", c, c + H))], last=False)
         to_list(v("QS", 0, 64), "ZS", "GS", 0, E)
         if t == 0:
-            cp("v", v("TB", 0, E), v("SRC", 0, E), bias=hk(8))
-            cp("a", v("TB", E, 2 * E), v("SRC", 0, E), bias=hk(16))
+            cp("v", v("SRC", 0, E), v("PT", 0, E), bias=hk(at(0) // 128))
+            cp("a", v("TB", 0, E), v("SRC", 0, E), bias=hk(8))
         else:
             state("a", t - 1, 0)
         message(t)
-        if t > 0:
-            own_columns("a", t - 1)
-        scatter(v("PT", 0, P), raw(t, 0), src(t, 0))
-        scatter(v("PT", 0, P), raw(t, 1), src(t, 1))
+        scatter(v("PT", 0, P), raw(t, 0, 2), v("SRC", 0, E) if t % 3 == 0 else v("TB", E * (t - 1), E * t))
+        if t == 1:
+            iota(v("HI", 0, E), [[1, E // 128], [0, 128]], at(3) // 128, 0)
+            dma("s", T.SRC[3::16, :], T.HI[3::16, :], [reg("HI", 0, E)], [reg("SRC", 0, E)])
+        if t == 2:
+            mark("MS", "MS", field, 199, 0.0)
+            mark("MS", "MS", field, -1, 1.0)
         if t == 0:
-            cp("a", v("TB", 2 * E, 3 * E), v("SRC", 0, E), bias=hk(24))
+            cp("a", v("TB", E, 2 * E), v("SRC", 0, E), bias=hk(16))
+            own_part(0)
             before("s", [], [reg("TB", 0, 2 * LW)])
             slot = lambda x: T.TB[x // 2::16, LW * (x % 2):LW * (x % 2) + LW]
             rs = lambda x: [reg("TB", LW * (x % 2), LW * (x % 2) + LW)]
@@ -305,62 +306,53 @@ def rank_program(g, core, T, topo):
             before("s", [reg("TD", 0, 4)], [])
             for x in peers:
                 dma("s", slot(x), T.TD[x], [reg("TD", x, x + 1)], rs(x), ordered=False)
+            iota(v("MS", 0, 128), [[0, 128]], 0, 0)
+            mark("MI", "MS", diag, 0, 1.0)
+            mark("MS", "MS", diag, 0, -1.0)
+            mark("MF", "MI", field, 199, 0.0)
+            mark("MS", "MS", field, 0, 0.0)
+            mark("MM", "MI", field, 0, 0.0)
             before("g", [reg("TB", 0, 2 * LW)], [])
             piece("r")
             dma("s", T.AB[:, 0:P], T.fld[:], [], [reg("AB", 0, P)])
             cp("a", col(WP), col(EQ + 3), scale=128.0, bias=col(EQ + 2))
             cp("a", col(NE1), col(EQ + 1), scale=-1.0, bias=1.0)
             cp("a", v("ZP", 0, 144), v("WK", 0, 144), scale=-128.0, bias=col(WP), func=Act.Relu)
-            cp("a", col(NE0), col(EQ), scale=-1.0, bias=1.0)
-            cp("a", col(NT), col(EQ + 1), bias=col(NP))
-            cp("a", v("WK", 144, 272), v("NI", 0, 128), bias=col(NP), func=Act.Abs)
-            cp("a", col(WS), col(EQ + 1), scale=2.0, bias=col(EQ))
-            cp("a", v("WK", 272, 400), v("NI", 0, 128), bias=col(NT), func=Act.Abs)
-            cp("a", col(WS + 1), col(WS), bias=-1.0)
-            cp("a", v("MM", 0, 128), v("WK", 144, 272), scale=-1.0, bias=col(NE0), func=Act.Relu)
         else:
-            c = at(t - 1)
-            mm([kept(0, "QF"), (v("QF", 0, H), v("MF", 0, 128), v("SP", c, c + H))])
+            mm([kept(0, "QF")], first=False)
             state("a", t - 1, 1)
+            o = 128 * me
+            cp("a", v("RC", H * (t - 1) + o, H * (t - 1) + o + 128), v("SP", c + o, c + o + 128))
             mm([(v("QG", 0, H), v("ZS", 15, 143), v("SP", c + H, c + E)), kept(1, "QG"),
                 (v("QG", 0, H), v("MS", 0, 128), v("RC", H * (t - 1), H * t))])
+            own_part(t)
+            if t == 1:
+                cp("a", col(NE0), col(EQ), scale=-1.0, bias=1.0)
             cp("a", v("AB", c, c + H), v("QF", 0, H))
         if t < 3:
             gather2("GP", v("PT", 0, P), lambda h: raw(t + 1, h))
             to_list(v("QP", 0, 64), "ZP", "GP", 0, E)
-        if t == 0:
-            cp("a", v("MF", 0, 128), v("WK", 144, 272), scale=-1.0, bias=col(NE1), func=Act.Relu)
-            cp("a", v("WK", 272, 400), v("WK", 272, 400), scale=-1.0, bias=1.0, func=Act.Relu)
-            cp("a", v("MS", 0, 128), v("WK", 272, 400), scale=col(WS + 1))
-        else:
+        if t > 0:
             cp("a", v("AB", c + H, c + E), v("QG", 0, H))
         if t == 3:
             to_list(v("QP", 0, 56), "ZP", "PT", 0, P // 2)
-            if FULL:
-                gather2("PRE", v("AB", 0, at(3)), lambda h: ptr(3, h))
-                for bank, m, q, o in LAST:
-                    mm([(v(bank, 0, 256), v("MM", 0, 128), v("PRE", o, o + 256))], last=False)
-            else:
-                to_list(v("QH", 0, 56), "ZP", "PT", P // 2, P)
+            state("a", 3, 1)
+            state("v", 3, 0, col(NE0))
+            for bank, m, q, o in LAST[1::2]:
+                mm([(v(bank, 0, 256), v("MM", 0, 128), v("PRE", o, o + 256))], last=False)
         lookup(t)
         if t < 3:
             cp("v", v("PTR", 64 * t + 64, 64 * t + 128), v("QP", 0, 64))
 
     c = at(3)
     cp("v", v("PTR", 256, 312), v("QP", 0, 56))
-    if FULL:
-        for bank, m, q, o in LAST:
-            mm([(v(bank, 0, 256), v(m, 0, 128), v("SP", c + o, c + o + 256))], first=False)
+    for bank, m, q, o in LAST:
+        mm([(v(bank, 0, 256), v(m, 0, 128), v("SP", c + o, c + o + 256))], first=q == "v")
+        if q == "v":
+            tt(v("AB", c + o, c + o + 256), v(bank, 0, 256), v("PRE", o, o + 256), Op.add)
+        else:
             cp(q, v("AB", c + o, c + o + 256), v(bank, 0, 256))
-        to_list(v("QH", 0, 56), "ZP", "PT", P // 2, P)
-    else:
-        own_columns("v", 3)
-        gather2("PRE", v("AB", 0, at(3)), lambda h: ptr(3, h))
-        mm([kept(0, "QF"), (v("QF", 0, H), v("MF", 0, 128), v("SP", c, c + H))])
-        mm([kept(1, "QG")], last=False)
-        cp("a", v("AB", c, c + H), v("QF", 0, H))
-        mm([(v("QG", 0, H), v("MS", 0, 128), v("RC", 3 * H, 4 * H))], first=False)
-        cp("a", v("AB", c + H, c + E), v("QG", 0, H))
+    to_list(v("QH", 0, 56), "ZP", "PT", P // 2, P)
     o = 0
     for w in OUT:
         if o <= P // 2 < o + w:

from concourse.bass import DstId, RemoteDMATransfer
from concourse.mybir import AluOpType as Op, ActivationFunctionType as Act

P, LW, E, H = 1792, 2304, 1024, 512
PIECES = {"r": (0, 512), "m1": (512, 1536), "m2": (1536, LW)}
OUT = [384, 512, 896]
S, B, F = "sbuf", "bfloat16", "float32"
SCRATCH = {
    "LI": (S, [128, 4, 32], "int32"), "LJ": (S, [128, 4, 32], "int32"), "LU": (S, [128, 4, 64], "uint16"),
    "NI": (S, [128, 144], F), "PI": (S, [128, 8], "int32"),
    "COL": (S, [128, 32], F), "HK": (S, [128, 48], B), "WK": (S, [128, 144], F), "ZS": (S, [128, 144], B),
    "ZP": (S, [128, 144], B), "MM": (S, [128, 128], B), "MF": (S, [128, 128], B), "MS": (S, [128, 128], B),
    "MI": (S, [128, 128], B), "PT": (S, [128, P], B), "SRC": (S, [128, E], B), "HI": (S, [128, E], B),
    "TB": (S, [128, 2 * LW], B), "LA": (S, [128, 4 * LW], B), "TD": ("dram", [4, 128, 144], B),
    "SP": (S, [128, P + 4 * E], B), "AB": (S, [128, P + 4 * E], B),
    "GS": (S, [128, E], B), "GP": (S, [128, E], B), "PRE": (S, [128, E], B),
    "MSG": (S, [128, 256], F), "RCV": (S, [128, 256], F), "OWN": (S, [128, 128], F), "IXF": (S, [128, 256], F),
    "IX": (S, [128, 256], "uint16"), "PTR": (S, [128, 368], "uint16"), "RC": (S, [128, 3 * H], B), "YO": (S, [128, P], F),
}
SCRATCH.update({"Q" + k: ("psum", [128, 512], F) for k in "SPFGHIJ"})
SEMAPHORES = (["qv", "qa", "qt", "qg", "sent", "tab", "laws"] + ["m%d" % t for t in range(4)] + ["c%d" % t for t in range(3)]
              + ["h" + k for k in PIECES] + ["d%d" % k for k in range(20)])


def engine_sets(src, dsts, topo):
    here = topo.cores_of(src)
    out, used = {}, []
    for group in ([d for d in dsts if d not in here], [d for d in dsts if d in here]):
        for k, d in enumerate(group):
            free = [e for e in topo.engines(src, d) if e not in used]
            n = 1
            while 2 * n * len(group) <= len(free):
                n *= 2
            out[d] = free[k * n:(k + 1) * n]
        used = used + sum([out[d] for d in group], [])
    return out


def law_route(src, cores, topo):
    near = [c for c in cores if c != src and c in topo.cores_of(src)]
    far = [c for c in cores if c not in topo.cores_of(src)]
    relay = [c for c in topo.cores_of(far[0]) if c not in cores and topo.die(c) == topo.die(src)][0]
    return near, relay, far


def fused(g, T, topo, core, sets, sem, src, dst):
    tr = []
    for d in sets:
        rid, pid = topo.addr(d, core)
        tr.append(RemoteDMATransfer(dst_ids=[DstId(rid=rid, pnc=pid)], dma_engine_mask=sum(1 << e for e in sets[d]),
                                    remote_sem=T.sem[sem(d)], src=src(d), dst=dst))
    g.remote_dma_fused(tr, local_sem=T.sem.sent)
    return sum(len(s) for s in sets.values())


def rank_program(g, core, T, topo):
    me = T.rank_of(core)
    cores = list(T.cores)
    routes = [law_route(c, cores, topo) for c in cores]
    if me is None:
        total = 0
        for x in range(4):
            near, relay, far = routes[x]
            if relay == core:
                for k, (a, b) in PIECES.items():
                    g.wait_ge(T.sem["h" + k], len(engine_sets(cores[x], near + [relay], topo)[core]))
                    part = T.LA[:, LW * x + a:LW * x + b]
                    total += fused(g, T, topo, core, engine_sets(core, far, topo), lambda d: "laws", lambda d: part, part)
        if total:
            g.wait_ge(T.sem.sent, total)
        return
    peers = [x for x in range(4) if x != me]
    sets = engine_sets(core, [cores[x] for x in peers], topo)
    arrive = sum(len(engine_sets(cores[x], [c for c in cores if c != cores[x]], topo)[core]) for x in peers)
    Q = {"v": g.vector, "a": g.scalar, "t": g.tensor, "g": g, "s": g.sync}
    count, waited, writes, reads, banks, ndma = {}, {}, [], [], [], [0]

    def v(name, a, b, step=1):
        return (T[name][:, a:b] if step == 1 else T[name][:, a:b:step], (name, a, b, step))

    def reg(name, a, b):
        return (name, a, b, 1)

    def hit(r, s):
        if r[0] != s[0] or (r[3] == s[3] > 1 and (r[1] - s[1]) % r[3]):
            return False
        return r[0][0] == "Q" or (r[1] < s[2] and s[1] < r[2])

    def wait(q, tok):
        if waited.get((q, tok[0]), 0) < tok[1]:
            waited[(q, tok[0])] = tok[1]
            Q[q].wait_ge(T.sem[tok[0]], tok[1])

    def before(q, rd, wr):
        need = {}
        for earlier, mine in ((writes, rd + wr), (reads, wr), ([b for b in banks if b[1][0] != "q" + q], rd)):
            for r, tok in earlier:
                if any(hit(r, s) for s in mine):
                    need[tok[0]] = max(need.get(tok[0], 0), tok[1])
        for s in sorted(need):
            wait(q, (s, need[s]))

    def note(tok, rd, wr):
        writes.extend((r, tok) for r in wr)
        reads.extend((r, tok) for r in rd)
        banks.extend((r, tok) for r in rd if r[0][0] == "Q")

    def done(q, ins, rd, wr):
        count["q" + q] = count.get("q" + q, 0) + 1
        ins.then_inc(T.sem["q" + q], 1)
        note(("q" + q, count["q" + q]), rd, wr)

    def regs(*xs):
        return [r for x in xs if isinstance(x, tuple) for r in x[1:]]

    def ap(x):
        return x[0] if isinstance(x, tuple) else x

    def ind(win, off):
        return (win[0].indirect(off[0]), win[1], off[1])

    def ts(out, in0, s1, s2, op0):
        before("v", regs(in0, s1, s2), regs(out))
        done("v", g.vector.tensor_scalar(ap(out), ap(in0), ap(s1), ap(s2), op0), regs(in0, s1, s2), regs(out))

    def tt(out, a, b, op):
        before("v", regs(a, b), regs(out))
        done("v", g.vector.tensor_tensor(ap(out), ap(a), ap(b), op), regs(a, b), regs(out))

    def cp(q, out, in_, scale=None, bias=None, func=Act.Identity):
        if q == "v" and scale is not None:
            return ts(out, in_, scale, None, Op.mult)
        if q == "v" and bias is not None:
            return ts(out, in_, bias, None, Op.add)
        rd = regs(in_, scale, bias)
        before(q, rd, regs(out))
        if q == "v":
            ins = g.vector.tensor_copy(ap(out), ap(in_))
        else:
            ins = g.scalar.activation(ap(out), ap(in_), func, 0.0 if bias is None else ap(bias),
                                      1.0 if scale is None else ap(scale))
        done(q, ins, rd, regs(out))

    def scatter(win, off, in_):
        before("v", regs(off, in_), regs(win))
        done("v", g.vector.tensor_copy(win[0].indirect(off[0]), in_[0]), regs(off, in_), regs(win))

    def mm(items, first=True, last=True):
        if first:
            before("t", [], regs(items[0][0]))
        for k, (out, lhs, rhs) in enumerate(items):
            before("t", regs(lhs, rhs), [])
            ins = g.tensor.matmul(out[0], lhs[0], rhs[0], first and k == 0, last and k == len(items) - 1)
        done("t", ins, regs(*[x for p in items for x in p[1:]]), [reg(items[0][0][1][0], 0, 512)])

    def to_list(out, z, name, a, b):
        mm([(out, v(z, 15 - i, 143 - i), v(name, a + i, b, 16)) for i in range(16)])

    def dma(q, out, in_, rd, wr, ordered=True):
        if ordered:
            before(q, rd, wr)
        s = "d%d" % ndma[0]
        ndma[0] += 1
        Q[q].dma_start(out, in_).then_inc(T.sem[s], 16)
        count[s] = 16
        note((s, 16), rd, wr)

    def piece(key):
        if key in PIECES:
            near, relay, far = routes[me]
            part = v("LA", LW * me + PIECES[key][0], LW * me + PIECES[key][1])
            before("g", regs(part), [])
            count["sent"] += fused(g, T, topo, core, engine_sets(core, near + [relay], topo),
                                   lambda d: "h" + key if d == relay else "laws", lambda d: part[0], part[0])

    def send(sem, src, dst, rd, landing):
        before("g", rd, [])
        count["sent"] = count.get("sent", 0) + fused(g, T, topo, core, sets, lambda d: sem, lambda d: src(cores.index(d)), dst)
        count[sem] = arrive
        note((sem, arrive), [], landing)
        piece(sem)

    def iota(out, pattern, base, mult):
        before("g", [], regs(out))
        done("g", g.iota(out[0], pattern, base, mult, allow_small_or_imprecise_dtypes=True), [], regs(out))

    def mark(out, in_, pattern, base, fill):
        out, in_ = v(out, 0, 128), v(in_, 0, 128)
        before("g", regs(in_), regs(out))
        done("g", g.affine_select(out[0], in_[0], pattern, Op.not_equal, fill, base, 1), regs(in_), regs(out))

    col = lambda k: v("COL", k, k + 1)
    hk = lambda k: v("HK", k, k + 1)
    raw = lambda t, h, n=1: (T.LU[:, t, 32 * h:32 * (h + n)], reg("LU", h, h + n))
    ptr = lambda t, h: raw(0, h) if t == 0 else v("PTR", 64 * t + 32 * h, 64 * t + 32 * h + 32)
    at = lambda t: P + E * t
    law = v("LA", LW * me, LW * me + LW)
    LAST = (("QF", "MF", "v", 0), ("QG", "MS", "a", H), ("QI", "MF", "v", 256), ("QJ", "MS", "a", H + 256))
    EQ, PM, NP, NC, W01, WP, NE1, NE0 = 0, 4, 8, 12, 13, 14, 16, 17
    diag, field = [[-1, 128]], [[-16, 8], [-200, 16]]

    dma("s", T.LI[:], T.la[:], [], [reg("LI", 0, 1)])
    dma("a", T.TD[me], T.law[1::16, :], [], [reg("TD", me, me + 1)])
    dma("a", T.LJ[:], T.lb[:], [], [reg("LJ", 0, 1)])
    done("v", g.vector.memset(T.SP[:, 0:P], 0.0), [], [reg("SP", 0, P)])
    done("g", g.iota(T.PI[:, 0:1], [[0, 1]], 0, 1), [], [reg("PI", 0, 1)])
    iota(v("NI", 0, 144), [[1, 144]], 0, 0)
    iota(v("COL", NP, NP + 2), [[-15, 2]], 0, -1)
    iota(v("TB", 3 * E, 3 * E + H), [[0, H]], 0, 0)
    dma("s", T.SP[0::16, 0:P], T.fld[0::16, :], [], [reg("SP", 0, P)])
    dma("s", T.TB[:, 2 * E:3 * E], T.law[:, 0:E], [], [reg("TB", 2 * E, 3 * E)])
    dma("s", law[0], T.law[:], [], regs(law))
    send("tab", lambda x: T.TD[me], T.TD[me], [reg("TD", me, me + 1)], [reg("TD", x, x + 1) for x in peers])
    iota(v("TB", 3 * E + H, 2 * LW), [[0, E]], 0, 0)
    ts(v("PI", 4, 5), v("PI", 0, 1), 15, None, Op.bitwise_and)
    cp("v", col(PM), v("PI", 4, 5))
    ts(v("COL", 0, 4), v("NI", 0, 4), col(PM), None, Op.is_equal)
    cp("a", v("HK", 0, 48), v("NI", 0, 48), scale=col(EQ + 3))
    cp("v", v("PT", 0, 128), v("NI", 0, 128), scale=col(EQ + 2))
    cp("a", col(NC), col(PM), bias=col(NP + 1))
    cp("a", col(W01), col(EQ), bias=col(EQ + 1))
    cp("a", v("WK", 0, 144), v("NI", 0, 144), bias=col(NC), func=Act.Abs)
    cp("a", v("ZS", 0, 144), v("WK", 0, 144), scale=-1.0, bias=col(W01), func=Act.Relu)
    for k in (1, 2, 4):
        cp("v", v("PT", 128 * k, 256 * k), v("PT", 0, 128 * k), bias=hk(k))
    cp("a", v("PT", E, P), v("PT", 0, P - E), bias=hk(8))
    cp("v", (T.LU[:, :, 0:32], reg("LU", 0, 1)), (T.LI[:], reg("LI", 0, 1)))
    cp("v", (T.LU[:, :, 32:64], reg("LU", 1, 2)), (T.LJ[:], reg("LJ", 0, 1)))

    def gather2(name, win, lists):
        for h, q in enumerate("va"):
            cp(q, v(name, H * h, H * h + H), ind(win, lists(h)))

    def message(t):
        b = 64 * t
        cp("a", v("MSG", b, b + 64, 2), v("QS", 32, 64))
        cp("a", v("MSG", b + 1, b + 64, 2), v("QS", 0, 32), scale=48.0, bias=float(LW * (me if t == 3 else me % 2)))
        send("m%d" % t, lambda x: T.MSG[:, b + 16 * x:b + 16 * x + 16], T.RCV[:, b + 16 * me:b + 16 * me + 16],
             [reg("MSG", b, b + 64)], [reg("RCV", b + 16 * x, b + 16 * x + 16) for x in peers])

    def own_part(t):
        b = 64 * t + 16 * me
        cp("a", v("RCV", b, b + 16), v("MSG", b, b + 16))
        cp("a", v("OWN", 32 * t, 32 * t + 32), v("QS", 0, 32), scale=48.0)

    def state(q, t, h, scale=None):
        cp(q, v("PRE", H * h, H * h + H), ind(v("AB", 0, at(t)), ptr(t, h)), scale=scale)

    def kept(h, bank):
        return (v(bank, 0, H), v("MM", 0, 128), v("PRE", H * h, H * h + H))

    def lookup(t):
        b, c = 64 * t, at(t)
        tt(v("IXF", b, b + 32), v("OWN", 32 * t, 32 * t + 32), v("RCV", b, b + 64, 2), Op.add)
        tt(v("IXF", b + 32, b + 64), v("RCV", b + 1, b + 64, 2), v("MSG", b, b + 64, 2), Op.add)
        cp("v", v("IX", b, b + 64), v("IXF", b, b + 64))
        second = lambda k: (v("SP", c + H + 256 * k, c + H + 256 * k + 256), v("IX", b + 32 + 16 * k, b + 48 + 16 * k))
        if t == 3:
            for k in range(2):
                cp("v", v("SP", c + 256 * k, c + 256 * k + 256), ind(law, v("IX", b + 16 * k, b + 16 * k + 16)))
                cp("a", second(k)[0], ind(v("LA", 0, 4 * LW), second(k)[1]))
            return
        if t == 0:
            for k, q in enumerate("va"):
                cp(q, v("SP", c + 256 * k, c + 256 * k + 256), ind(law, v("IX", b + 16 * k, b + 16 * k + 16)), scale=col(NE1))
        else:
            cp("v", v("SP", c, c + H), ind(law, v("IX", b, b + 32)), scale=col(NE1))
        for k, q in enumerate("va" if t == 0 else "aa"):
            cp(q, second(k)[0], ind(v("TB", 0, 2 * LW), second(k)[1]), scale=col(EQ + k))
        send("c%d" % t, lambda x: T.SP[:, c + 128 * x:c + 128 * x + 128], T.RC[:, H * t + 128 * me:H * t + 128 * me + 128],
             [reg("SP", c, c + H)], [reg("RC", H * t + 128 * x, H * t + 128 * x + 128) for x in peers])

    n = 0
    for x in peers:
        near, relay, far = routes[x]
        n += len(engine_sets(cores[x], near + [relay], topo)[core] if core in near else engine_sets(relay, far, topo)[core])
    count["laws"] = n * len(PIECES)
    note(("laws", count["laws"]), [], [reg("LA", LW * x, LW * x + LW) for x in peers])

    for t in range(4):
        c = at(t - 1)
        gather2("GS", v("SP", 0, at(t)), lambda h: ptr(t, h))
        if t > 0:
            mm([(v("QF", 0, H), v("MF", 0, 128), v("SP", c, c + H))], last=False)
        to_list(v("QS", 0, 64), "ZS", "GS", 0, E)
        if t == 0:
            cp("v", v("SRC", 0, E), v("PT", 0, E), bias=hk(at(0) // 128))
            cp("a", v("TB", 0, E), v("SRC", 0, E), bias=hk(8))
        else:
            state("a", t - 1, 0)
        message(t)
        scatter(v("PT", 0, P), raw(t, 0, 2), v("SRC", 0, E) if t % 3 == 0 else v("TB", E * (t - 1), E * t))
        if t == 1:
            iota(v("HI", 0, E), [[1, E // 128], [0, 128]], at(3) // 128, 0)
            dma("s", T.SRC[3::16, :], T.HI[3::16, :], [reg("HI", 0, E)], [reg("SRC", 0, E)])
        if t == 2:
            mark("MS", "MS", field, 199, 0.0)
            mark("MS", "MS", field, -1, 1.0)
        if t == 0:
            cp("a", v("TB", E, 2 * E), v("SRC", 0, E), bias=hk(16))
            own_part(0)
            before("s", [], [reg("TB", 0, 2 * LW)])
            slot = lambda x: T.TB[x // 2::16, LW * (x % 2):LW * (x % 2) + LW]
            rs = lambda x: [reg("TB", LW * (x % 2), LW * (x % 2) + LW)]
            dma("s", slot(me), T.law[1::16, :], [], rs(me), ordered=False)
            before("s", [reg("TD", 0, 4)], [])
            for x in peers:
                dma("s", slot(x), T.TD[x], [reg("TD", x, x + 1)], rs(x), ordered=False)
            iota(v("MS", 0, 128), [[0, 128]], 0, 0)
            mark("MI", "MS", diag, 0, 1.0)
            mark("MS", "MS", diag, 0, -1.0)
            mark("MF", "MI", field, 199, 0.0)
            mark("MS", "MS", field, 0, 0.0)
            mark("MM", "MI", field, 0, 0.0)
            before("g", [reg("TB", 0, 2 * LW)], [])
            piece("r")
            dma("s", T.AB[:, 0:P], T.fld[:], [], [reg("AB", 0, P)])
            cp("a", col(WP), col(EQ + 3), scale=128.0, bias=col(EQ + 2))
            cp("a", col(NE1), col(EQ + 1), scale=-1.0, bias=1.0)
            cp("a", v("ZP", 0, 144), v("WK", 0, 144), scale=-128.0, bias=col(WP), func=Act.Relu)
        else:
            mm([kept(0, "QF")], first=False)
            state("a", t - 1, 1)
            o = 128 * me
            cp("a", v("RC", H * (t - 1) + o, H * (t - 1) + o + 128), v("SP", c + o, c + o + 128))
            mm([(v("QG", 0, H), v("ZS", 15, 143), v("SP", c + H, c + E)), kept(1, "QG"),
                (v("QG", 0, H), v("MS", 0, 128), v("RC", H * (t - 1), H * t))])
            own_part(t)
            if t == 1:
                cp("a", col(NE0), col(EQ), scale=-1.0, bias=1.0)
            cp("a", v("AB", c, c + H), v("QF", 0, H))
        if t < 3:
            gather2("GP", v("PT", 0, P), lambda h: raw(t + 1, h))
            to_list(v("QP", 0, 64), "ZP", "GP", 0, E)
        if t > 0:
            cp("a", v("AB", c + H, c + E), v("QG", 0, H))
        if t == 3:
            to_list(v("QP", 0, 56), "ZP", "PT", 0, P // 2)
            state("a", 3, 1)
            state("v", 3, 0, col(NE0))
            for bank, m, q, o in LAST[1::2]:
                mm([(v(bank, 0, 256), v("MM", 0, 128), v("PRE", o, o + 256))], last=False)
        lookup(t)
        if t < 3:
            cp("v", v("PTR", 64 * t + 64, 64 * t + 128), v("QP", 0, 64))

    c = at(3)
    cp("v", v("PTR", 256, 312), v("QP", 0, 56))
    for bank, m, q, o in LAST:
        mm([(v(bank, 0, 256), v(m, 0, 128), v("SP", c + o, c + o + 256))], first=q == "v")
        if q == "v":
            tt(v("AB", c + o, c + o + 256), v(bank, 0, 256), v("PRE", o, o + 256), Op.add)
        else:
            cp(q, v("AB", c + o, c + o + 256), v(bank, 0, 256))
    to_list(v("QH", 0, 56), "ZP", "PT", P // 2, P)
    o = 0
    for w in OUT:
        if o <= P // 2 < o + w:
            cp("v", v("PTR", 312, 368), v("QH", 0, 56))
        for q, a in (("v", o), ("a", o + w // 2)):
            cp(q, v("YO", a, a + w // 2), ind(v("AB", 0, at(4)), v("PTR", 256 + a // 16, 256 + (a + w // 2) // 16)))
        dma("s", T.y[:, o:o + w], T.YO[:, o:o + w], [reg("YO", o, o + w)], [])
        o += w
    for s in sorted(count):
        wait("g", (s, count[s]))
